import numpy as np
import ml_dtypes


def mxq(x, axis, fmt="e4m3"):
    dtype, down = {"e4m3": (ml_dtypes.float8_e4m3fn, 7), "e5m2": (ml_dtypes.float8_e5m2, 14)}[fmt]
    v = np.moveaxis(np.asarray(x, np.float32).astype(ml_dtypes.bfloat16).astype(np.float64), axis, -1)
    blocks = v.reshape(v.shape[:-1] + (-1, 32))
    amax = np.abs(blocks).max(-1, keepdims=True)
    byte = np.maximum(np.where(amax > 0, np.frexp(amax)[1] - 1 + 127, 0) - down, 1)
    scale = np.exp2(byte - 127.0)
    codes = (blocks / scale).astype(np.float32).astype(dtype).astype(np.float64)
    return np.moveaxis((codes * scale).reshape(v.shape), -1, axis)


WIDE = False


def mx_kscale(k):
    if not WIDE:
        return np.ones(k)
    levels = np.array([10, -10, 5, -5, 0])
    if k % 512:
        return np.exp2(np.random.permutation(np.resize(levels, k // 32))).repeat(32)
    a = np.empty((k // 512, 16))
    for p in range(k // 512):
        a[p, :8] = np.random.permutation(np.resize(levels, 8))
        for g in range(8):
            far = levels[np.abs(levels - a[p, g]) >= 10]
            a[p, g + 8] = far[np.random.randint(len(far))]
    return np.exp2(a.ravel()).repeat(32)


def f64(x):
    return np.asarray(x).astype(np.float64)


def striped(idx):
    return np.tile(np.asarray(idx).reshape(-1, 16).T, (8, 1)).astype(np.uint16)


def unstriped(offs):
    return offs[:16].T.reshape(-1).astype(np.int64)


E2M1 = np.array([0.0, 0.5, 1.0, 1.5, 2.0, 3.0, 4.0, 6.0, -0.0, -0.5, -1.0, -1.5, -2.0, -3.0, -4.0, -6.0])


def pack_weight(w, fmt):
    k, n = w.shape
    w = f64(np.asarray(w, np.float32).astype(ml_dtypes.bfloat16)).reshape(k // 32, 32, n)
    amax = np.abs(w).max(1)
    if fmt == "e4m3":
        byte = np.frexp(amax)[1] - 1 + 127 - 7
    else:
        mant, ex = np.frexp(amax / 6.0)
        byte = np.where(mant > 0.5, ex, ex - 1) + 127
    byte = np.clip(np.where(amax > 0, byte, 1), 1, 254)
    scaled = (w * np.exp2(127.0 - byte)[:, None, :]).reshape(k, n).astype(np.float32)
    by_word = np.ascontiguousarray(scaled.reshape(k // 512, 128, 4, n).transpose(0, 1, 3, 2))
    if fmt == "e4m3":
        words = by_word.astype(ml_dtypes.float8_e4m3fn).view(np.uint8)
    else:
        c = by_word.astype(ml_dtypes.float4_e2m1fn).view(np.uint8) & 0xF
        words = (c[..., 0::2] | (c[..., 1::2] << 4)).reshape(k // 512, 128, 2 * n)
    return np.ascontiguousarray(words), np.ascontiguousarray(byte.astype(np.uint8).reshape(k // 512, 16, n))


def unpack_weight(words, scales, fmt):
    g, _, n = scales.shape
    words = np.ascontiguousarray(words).reshape(g, 128, n, -1)
    if fmt == "e4m3":
        vals = words.view(ml_dtypes.float8_e4m3fn).astype(np.float64)
    else:
        nib = np.empty((g, 128, n, 4), np.uint8)
        nib[..., 0::2] = words & 0xF
        nib[..., 1::2] = words >> 4
        vals = E2M1[nib]
    vals = vals * np.repeat(np.exp2(scales.astype(np.float64) - 127.0), 8, axis=1)[..., None]
    return vals.transpose(0, 1, 3, 2).reshape(g * 512, n)


D, E, T, I, Q = 512, 512, 2048, 512, 128


def setup_inputs():
    n = np.random.standard_normal
    idx = np.random.permutation(T)[:I]
    fd = mx_kscale(D)
    fe = mx_kscale(E)
    keysp = pack_weight(n((D, T)) / fd[:, None], "e4m3")
    valsp = pack_weight(n((E, T)) / fe[:, None], "e4m3")
    return {
        "query": (n((D, Q)) * 1.0 / np.sqrt(D) * fd[:, None]).astype(np.float32),
        "keys_words": keysp[0],
        "keys_scales": keysp[1],
        "floor": (np.random.uniform(0.05, 0.3, (Q, 1))).astype(np.float32),
        "reserve": (np.random.uniform(20.0, 100.0, (Q, 1))).astype(np.float32),
        "gout": (n((E, Q)) * 1 / np.sqrt(E) * fe[:, None]).astype(np.float32),
        "vals_words": valsp[0],
        "vals_scales": valsp[1],
        "base": (0.5 * n((Q, I))).astype(np.float32),
        "offs": striped(idx),
    }


def reference(query, keys_words, keys_scales, floor, reserve, gout, vals_words, vals_scales, base, offs):
    idx = unstriped(offs)
    keysu = unpack_weight(keys_words, keys_scales, "e4m3")
    valsu = unpack_weight(vals_words, vals_scales, "e4m3")
    queryq = mxq(f64(query), 0, "e4m3")
    keysidxg = keysu[:, idx]
    a = queryq.T @ keysidxg
    p = np.square(a) + f64(floor)
    z = np.sum(p, axis=1, keepdims=True) + f64(reserve)
    goutq = mxq(f64(gout), 0, "e4m3")
    valsidxg = valsu[:, idx]
    c0 = goutq.T @ valsidxg
    dz = np.sum(c0 * p / np.square(z) * (-1.0), axis=1, keepdims=True)
    dp = c0 / z + dz
    da = dp * a * 2.0
    hda = da * 512.0 * 2.0 * 512.0
    hdp = hda * 2.0 * a
    hdz = np.sum(hdp, axis=1, keepdims=True)
    hz = np.sum(hdp * c0 / np.square(z) * (-1.0), axis=1, keepdims=True) + np.sum(hdz * (-1.0) * c0 * p / np.square(np.square(z)) * (-1.0), axis=1, keepdims=True) * z * 2.0
    hp = hdz * (-1.0) / np.square(z) * c0 + hz
    ha = hda * 2.0 * dp + hp * a * 2.0
    y = ha + f64(base)
    return y

@@ -1,0 +1,194 @@
+from contextlib import ExitStack
+
+import concourse.mybir as mybir
+
+D, E, T, I, Q = 512, 512, 2048, 512, 128
+FLOPS = 2 * Q * I * (D + E)
+
+F32 = mybir.dt.float32
+BF16 = mybir.dt.bfloat16
+I32 = mybir.dt.int32
+U32 = mybir.dt.uint32
+U16 = mybir.dt.uint16
+U8 = mybir.dt.uint8
+FP8X4 = mybir.dt.float8_e4m3fn_x4
+MULT = mybir.AluOpType.mult
+ADD = mybir.AluOpType.add
+SUB = mybir.AluOpType.subtract
+ACT = mybir.ActivationFunctionType
+
+P = 128
+PACK = 4
+HALF = I // 2
+LIST_ROWS = 16
+KEY_ROW, VAL_ROW = 0, 4
+PAIRS = 16
+ONE = 16
+SHIFT = slice(17, 21)
+SHIFT_S = slice(17, 19)
+GAIN = 24
+COEFS = 25
+TERMS = I + PAIRS + 1
+
+
+def col(tile, j):
+    return tile[:, j : j + 1]
+
+
+def tile_attend_gpsquareshares_kernel(tc, query, keys_words, keys_scales, floor, reserve, gout, vals_words, vals_scales, base, offs, out):
+    nc = tc.nc
+    with ExitStack() as ctx:
+        sb = ctx.enter_context(tc.tile_pool(name="sb", bufs=1))
+        psum = ctx.enter_context(tc.psum_pool(name="psum", bufs=1))
+
+        offsets = sb.tile([P, I // LIST_ROWS], U16, name="offsets")
+        nc.sync.dma_start(offsets[:], offs)
+
+        def load_scales(name, src, row, clear):
+            plane = sb.tile([P, T], U8, name=name)
+            clear.memset(plane[:].bitcast(I32), 0)
+            for quad in range(4):
+                nc.sync.dma_start(plane[32 * quad + row : 32 * quad + row + 4, :].bitcast(I32), src[0, 4 * quad : 4 * quad + 4, :].bitcast(I32))
+            return plane
+
+        def load_words(name, src):
+            words = sb.tile([P, T], I32, name=name, tag=name)
+            nc.sync.dma_start(words[:], src[0].rearrange("p n t -> p (n t)").bitcast(I32))
+            return words
+
+        def load_rows(name, src):
+            raw = sb.tile([P, PACK, Q], F32, name=name)
+            nc.sync.dma_start(raw[:], src.rearrange("(p j) q -> p j q", j=PACK))
+            return raw
+
+        query_raw = load_rows("query_raw", query)
+        key_plane = load_scales("key_plane", keys_scales, KEY_ROW, nc.gpsimd)
+        key_words = load_words("key_words", keys_words)
+        val_plane = load_scales("val_plane", vals_scales, VAL_ROW, nc.vector)
+        gout_raw = load_rows("gout_raw", gout)
+        val_words = load_words("val_words", vals_words)
+        base_sb = sb.tile([P, I], F32, name="base_sb")
+        nc.sync.dma_start(base_sb[:], base)
+        f = sb.tile([P, 1], F32, name="f")
+        nc.gpsimd.dma_start(f[:], floor)
+        res = sb.tile([P, 1], F32, name="res")
+        nc.gpsimd.dma_start(res[:], reserve)
+
+        k1 = sb.tile([P, 4, 4], F32, name="k1")
+        nc.vector.memset(k1[:], -3.0)
+        nc.vector.memset(k1[:, 0:2, 0:2], -2.0)
+        nc.vector.memset(k1[:, 2:4, 2:4], -4.0)
+        n0 = sb.tile([P, COEFS], F32, name="n0")
+        n1 = sb.tile([P, COEFS], F32, name="n1")
+        n2 = sb.tile([P, COEFS], F32, name="n2")
+        f4 = sb.tile([P, 4], F32, name="f4")
+        n0_pairs = n0[:, :PAIRS].rearrange("p (a b) -> p a b", a=4)
+        nc.vector.memset(n0[:], 0.0)
+        nc.vector.memset(n0_pairs[:, 0:2, 0:2], -0.5)
+        nc.vector.memset(col(n0, ONE), 1.0)
+        nc.vector.memset(n1[:, PAIRS:], 0.0)
+        nc.vector.memset(n1[:, SHIFT_S], 0.5)
+        nc.vector.memset(n2[:, PAIRS:], 0.0)
+        nc.vector.memset(col(n2, GAIN), float(2**21))
+        nc.vector.memset(f4[:, 0:2], 0.5)
+        w = sb.tile([P, 1], F32, name="w")
+        wff = sb.tile([P, 4, 4], F32, name="wff")
+        wf4 = n2[:, SHIFT]
+        nc.gpsimd.tensor_scalar(w[:], f[:], float(I), res[:], MULT, ADD)
+        nc.gpsimd.tensor_scalar(f4[:, 2:4], f4[:, 0:2], f[:], 2.0, MULT, MULT)
+        nc.gpsimd.tensor_scalar(n0_pairs[:, 2:4, 2:4], f[:].unsqueeze(2).to_broadcast([P, 2, 2]), f[:], 3.0, MULT, MULT)
+        nc.gpsimd.tensor_scalar(wf4, f4[:], w[:], 1.0, MULT, MULT)
+
+        def outer(dst, rows, cols):
+            nc.gpsimd.tensor_tensor(dst, rows.unsqueeze(2).to_broadcast([P, 4, 4]), cols.unsqueeze(1).to_broadcast([P, 4, 4]), MULT)
+
+        outer(wff[:], wf4, f4[:])
+        nc.gpsimd.tensor_tensor(n1[:, :PAIRS], wff[:].rearrange("p a b -> p (a b)"), k1[:].rearrange("p a b -> p (a b)"), MULT)
+        outer(n2[:, :PAIRS].rearrange("p (a b) -> p a b", a=4), wf4, wf4)
+
+        def gather(dst, window, first, count):
+            nc.vector.tensor_copy(dst, window.indirect(offsets[:, first // LIST_ROWS : (first + count) // LIST_ROWS]))
+
+        def cast(name, raw):
+            grouped = sb.tile([P, Q, PACK], BF16, name=name, align_bytes=64)
+            nc.scalar.activation(grouped[:], raw[:].rearrange("p j q -> p q j"), ACT.Copy)
+            return grouped
+
+        def quantise(name, grouped):
+            codes = sb.tile([P, Q], U32, name=name + "_codes", align_bytes=64)
+            scales = sb.tile([P, Q], U8, name=name + "_scales", align_bytes=64)
+            nc.vector.quantize_mx(out=codes[:].bitcast(FP8X4), scales=scales[:], in_=grouped[:].rearrange("p q j -> p (q j)"))
+            return codes, scales
+
+        def product(dst, lhs, words, plane, row):
+            nc.tensor.matmul_mx(out=dst, lhsT=lhs[0][:].bitcast(FP8X4), lhsT_scale=lhs[1][:], rhs=words.bitcast(FP8X4), rhs_scale=plane[row:P, :], start=True, stop=True)
+
+        key_bytes = sb.tile([P, I], U8, name="key_bytes", align_bytes=64)
+        key_codes = sb.tile([P, I], U32, name="key_codes", align_bytes=64)
+        val_bytes = sb.tile([P, I], U8, name="val_bytes", align_bytes=64)
+        query_bf = cast("query_bf", query_raw)
+        gout_bf = cast("gout_bf", gout_raw)
+        gather(key_bytes[:], key_plane[:], 0, I)
+        query_mx = quantise("query", query_bf)
+        gather(key_codes[:], key_words[:].bitcast(U32), 0, I)
+        a = psum.tile([P, I], F32, name="a")
+        product(a[:], query_mx, key_codes[:], key_bytes[:], KEY_ROW)
+        gather(val_bytes[:], val_plane[:], 0, I)
+        gout_mx = quantise("gout", gout_bf)
+
+        s = sb.tile([P, I], F32, name="s")
+        s0 = sb.tile([P, 1], F32, name="s0")
+        nc.scalar.activation(s[:], a[:], ACT.Square, accum_out=s0[:])
+        z = sb.tile([P, 1], F32, name="z")
+        nc.scalar.activation(z[:], s0[:], ACT.Identity, bias=w[:])
+
+        halves = [slice(h * HALF, (h + 1) * HALF) for h in range(2)]
+        val_codes = [sb.tile([P, HALF], U32, name="val_codes%d" % h, align_bytes=64) for h in range(2)]
+        for h in range(2):
+            gather(val_codes[h][:], val_words[:].bitcast(U32), h * HALF, HALF)
+        c_v = [psum.tile([P, HALF], F32, name="c%d" % h) for h in range(2)]
+        c_twin = psum.tile([P, HALF], F32, name="c_twin")
+        c_s = [c_v[0], c_twin]
+        product(c_v[0][:], gout_mx, val_codes[0][:], val_bytes[:, halves[0]], VAL_ROW)
+        product(c_v[1][:], gout_mx, val_codes[1][:], val_bytes[:, halves[1]], VAL_ROW)
+        product(c_twin[:], gout_mx, val_codes[1][:], val_bytes[:, halves[1]], VAL_ROW)
+
+        r = sb.tile([P, 1], F32, name="r", tag="val_words")
+        q1 = sb.tile([P, COEFS], F32, name="q1")
+        u = sb.tile([P, I + COEFS], F32, name="u")
+        q2 = u[:, I:]
+        sums = sb.tile([P, 4], F32, name="sums")
+        c = sb.tile([P, TERMS], F32, name="c")
+        nc.vector.reciprocal(r[:], z[:])
+        for h in range(2):
+            nc.vector.scalar_tensor_tensor(u[:, halves[h]], c_v[h][:], 2.0, s[:, halves[h]], MULT, MULT, accum_out=col(sums, h))
+            nc.scalar.activation(c[:, halves[h]], c_s[h][:], ACT.Copy, accum_out=col(sums, 2 + h))
+            if h == 0:
+                nc.vector.scalar_tensor_tensor(q1[:], n2[:], r[:], n1[:], MULT, ADD)
+                nc.vector.scalar_tensor_tensor(q2, q1[:], r[:], n0[:], MULT, ADD)
+        level_terms = sb.tile([P, TERMS], F32, name="level_terms")
+        nc.vector.scalar_tensor_tensor(level_terms[:, :HALF], c[:, :HALF], 1.0, u[:, :HALF], MULT, MULT, accum_out=col(c, I + ONE))
+        nc.vector.scalar_tensor_tensor(
+            c[:, I : I + PAIRS].rearrange("p (a b) -> p a b", a=4),
+            sums[:].unsqueeze(2).to_broadcast([P, 4, 4]),
+            r[:],
+            sums[:].unsqueeze(1).to_broadcast([P, 4, 4]),
+            MULT,
+            MULT,
+        )
+        shift = sb.tile([P, 1], F32, name="shift")
+        shift_terms = sb.tile([P, 4], F32, name="shift_terms")
+        nc.vector.scalar_tensor_tensor(shift_terms[:], sums[:], r[:], q1[:, SHIFT], MULT, MULT, accum_out=shift[:])
+        level = sb.tile([P, 1], F32, name="level")
+        nc.vector.scalar_tensor_tensor(level_terms[:, HALF:], c[:, HALF:], r[:], u[:, HALF:TERMS], MULT, MULT, accum_out=level[:])
+
+        x = []
+        for h in range(2):
+            t = sb.tile([P, HALF], F32, name="t%d" % h)
+            nc.scalar.activation(t[:], c[:, halves[h]], ACT.Square, bias=shift[:], scale=-1.0)
+            x.append(sb.tile([P, HALF], F32, name="x%d" % h))
+            nc.vector.scalar_tensor_tensor(x[h][:], t[:], level[:], a[:, halves[h]], SUB, MULT)
+        for h in range(2):
+            y = sb.tile([P, HALF], F32, name="y%d" % h)
+            nc.vector.scalar_tensor_tensor(y[:], x[h][:], col(q2, GAIN), base_sb[:, halves[h]], MULT, ADD)
+            (nc.sync, nc.scalar)[h].dma_start(out[:, halves[h]], y[:])

@@ -24,8 +24,8 @@ LIST_ROWS = 16
 KEY_ROW, VAL_ROW = 0, 4
 PAIRS = 16
 ONE = 16
-SHIFT = slice(17, 21)
-SHIFT_S = slice(17, 19)
+SHIFT = slice(18, 22)
+SHIFT_S = slice(18, 20)
 GAIN = 24
 COEFS = 25
 TERMS = I + PAIRS + 1
@@ -51,24 +51,21 @@ def tile_attend_gpsquareshares_kernel(tc, query, keys_words, keys_scales, floor,
                 nc.sync.dma_start(plane[32 * quad + row : 32 * quad + row + 4, :].bitcast(I32), src[0, 4 * quad : 4 * quad + 4, :].bitcast(I32))
             return plane
 
-        def load_words(name, src):
-            words = sb.tile([P, T], I32, name=name, tag=name)
+        def load_words(name, src, tag):
+            words = sb.tile([P, T], I32, name=name, tag=tag)
             nc.sync.dma_start(words[:], src[0].rearrange("p n t -> p (n t)").bitcast(I32))
             return words
 
         def load_rows(name, src):
-            raw = sb.tile([P, PACK, Q], F32, name=name)
+            raw = sb.tile([P, PACK, Q], F32, name=name, tag=name)
             nc.sync.dma_start(raw[:], src.rearrange("(p j) q -> p j q", j=PACK))
             return raw
 
         query_raw = load_rows("query_raw", query)
-        key_plane = load_scales("key_plane", keys_scales, KEY_ROW, nc.gpsimd)
-        key_words = load_words("key_words", keys_words)
-        val_plane = load_scales("val_plane", vals_scales, VAL_ROW, nc.vector)
         gout_raw = load_rows("gout_raw", gout)
-        val_words = load_words("val_words", vals_words)
-        base_sb = sb.tile([P, I], F32, name="base_sb")
-        nc.sync.dma_start(base_sb[:], base)
+        key_plane = load_scales("key_plane", keys_scales, KEY_ROW, nc.gpsimd)
+        key_words = load_words("key_words", keys_words, "key_words")
+        val_plane = load_scales("val_plane", vals_scales, VAL_ROW, nc.vector)
         f = sb.tile([P, 1], F32, name="f")
         nc.gpsimd.dma_start(f[:], floor)
         res = sb.tile([P, 1], F32, name="res")
@@ -96,7 +93,6 @@ def tile_attend_gpsquareshares_kernel(tc, query, keys_words, keys_scales, floor,
         wf4 = n2[:, SHIFT]
         nc.gpsimd.tensor_scalar(w[:], f[:], float(I), res[:], MULT, ADD)
         nc.gpsimd.tensor_scalar(f4[:, 2:4], f4[:, 0:2], f[:], 2.0, MULT, MULT)
-        nc.gpsimd.tensor_scalar(n0_pairs[:, 2:4, 2:4], f[:].unsqueeze(2).to_broadcast([P, 2, 2]), f[:], 3.0, MULT, MULT)
         nc.gpsimd.tensor_scalar(wf4, f4[:], w[:], 1.0, MULT, MULT)
 
         def outer(dst, rows, cols):
@@ -105,6 +101,7 @@ def tile_attend_gpsquareshares_kernel(tc, query, keys_words, keys_scales, floor,
         outer(wff[:], wf4, f4[:])
         nc.gpsimd.tensor_tensor(n1[:, :PAIRS], wff[:].rearrange("p a b -> p (a b)"), k1[:].rearrange("p a b -> p (a b)"), MULT)
         outer(n2[:, :PAIRS].rearrange("p (a b) -> p a b", a=4), wf4, wf4)
+        nc.gpsimd.tensor_scalar(n0_pairs[:, 2:4, 2:4], f[:].unsqueeze(2).to_broadcast([P, 2, 2]), f[:], 3.0, MULT, MULT)
 
         def gather(dst, window, first, count):
             nc.vector.tensor_copy(dst, window.indirect(offsets[:, first // LIST_ROWS : (first + count) // LIST_ROWS]))
@@ -128,13 +125,16 @@ def tile_attend_gpsquareshares_kernel(tc, query, keys_words, keys_scales, floor,
         val_bytes = sb.tile([P, I], U8, name="val_bytes", align_bytes=64)
         query_bf = cast("query_bf", query_raw)
         gout_bf = cast("gout_bf", gout_raw)
+        val_words = load_words("val_words", vals_words, "query_raw")
         gather(key_bytes[:], key_plane[:], 0, I)
         query_mx = quantise("query", query_bf)
+        gout_mx = quantise("gout", gout_bf)
         gather(key_codes[:], key_words[:].bitcast(U32), 0, I)
+        base_sb = sb.tile([P, I], F32, name="base_sb", tag="key_words")
+        nc.sync.dma_start(base_sb[:], base)
         a = psum.tile([P, I], F32, name="a")
         product(a[:], query_mx, key_codes[:], key_bytes[:], KEY_ROW)
         gather(val_bytes[:], val_plane[:], 0, I)
-        gout_mx = quantise("gout", gout_bf)
 
         s = sb.tile([P, I], F32, name="s")
         s0 = sb.tile([P, 1], F32, name="s0")
@@ -153,7 +153,7 @@ def tile_attend_gpsquareshares_kernel(tc, query, keys_words, keys_scales, floor,
         product(c_v[1][:], gout_mx, val_codes[1][:], val_bytes[:, halves[1]], VAL_ROW)
         product(c_twin[:], gout_mx, val_codes[1][:], val_bytes[:, halves[1]], VAL_ROW)
 
-        r = sb.tile([P, 1], F32, name="r", tag="val_words")
+        r = sb.tile([P, 1], F32, name="r", tag="query_raw")
         q1 = sb.tile([P, COEFS], F32, name="q1")
         u = sb.tile([P, I + COEFS], F32, name="u")
         q2 = u[:, I:]

@@ -1,3 +1,4 @@
+import math
 from contextlib import ExitStack
 
 import concourse.mybir as mybir
@@ -71,15 +72,12 @@ def tile_attend_gpsquareshares_kernel(tc, query, keys_words, keys_scales, floor,
         res = sb.tile([P, 1], F32, name="res")
         nc.gpsimd.dma_start(res[:], reserve)
 
-        k1 = sb.tile([P, 4, 4], F32, name="k1")
-        nc.vector.memset(k1[:], -3.0)
-        nc.vector.memset(k1[:, 0:2, 0:2], -2.0)
-        nc.vector.memset(k1[:, 2:4, 2:4], -4.0)
         n0 = sb.tile([P, COEFS], F32, name="n0")
         n1 = sb.tile([P, COEFS], F32, name="n1")
         n2 = sb.tile([P, COEFS], F32, name="n2")
-        f4 = sb.tile([P, 4], F32, name="f4")
-        n0_pairs = n0[:, :PAIRS].rearrange("p (a b) -> p a b", a=4)
+        rows = sb.tile([P, 3, 4], F32, name="rows")
+        floor_factor = sb.tile([P, 3, 2], F32, name="floor_factor")
+        n0_pairs, n1_pairs, n2_pairs = [n[:, :PAIRS].rearrange("p (a b) -> p a b", a=4) for n in (n0, n1, n2)]
         nc.vector.memset(n0[:], 0.0)
         nc.vector.memset(n0_pairs[:, 0:2, 0:2], -0.5)
         nc.vector.memset(col(n0, ONE), 1.0)
@@ -87,21 +85,9 @@ def tile_attend_gpsquareshares_kernel(tc, query, keys_words, keys_scales, floor,
         nc.vector.memset(n1[:, SHIFT_S], 0.5)
         nc.vector.memset(n2[:, PAIRS:], 0.0)
         nc.vector.memset(col(n2, GAIN), float(2**21))
-        nc.vector.memset(f4[:, 0:2], 0.5)
-        w = sb.tile([P, 1], F32, name="w")
-        wff = sb.tile([P, 4, 4], F32, name="wff")
-        wf4 = n2[:, SHIFT]
-        nc.gpsimd.tensor_scalar(w[:], f[:], float(I), res[:], MULT, ADD)
-        nc.gpsimd.tensor_scalar(f4[:, 2:4], f4[:, 0:2], f[:], 2.0, MULT, MULT)
-        nc.gpsimd.tensor_scalar(wf4, f4[:], w[:], 1.0, MULT, MULT)
-
-        def outer(dst, rows, cols):
-            nc.gpsimd.tensor_tensor(dst, rows.unsqueeze(2).to_broadcast([P, 4, 4]), cols.unsqueeze(1).to_broadcast([P, 4, 4]), MULT)
-
-        outer(wff[:], wf4, f4[:])
-        nc.gpsimd.tensor_tensor(n1[:, :PAIRS], wff[:].rearrange("p a b -> p (a b)"), k1[:].rearrange("p a b -> p (a b)"), MULT)
-        outer(n2[:, :PAIRS].rearrange("p (a b) -> p a b", a=4), wf4, wf4)
-        nc.gpsimd.tensor_scalar(n0_pairs[:, 2:4, 2:4], f[:].unsqueeze(2).to_broadcast([P, 2, 2]), f[:], 3.0, MULT, MULT)
+        for j, (first, second) in enumerate(((0.5, 1.0), (-1.0, -3.0), (-1.5, -4.0))):
+            nc.vector.memset(rows[:, j, 0:2], first)
+            nc.vector.memset(floor_factor[:, j, :], second)
 
         def gather(dst, window, first, count):
             nc.vector.tensor_copy(dst, window.indirect(offsets[:, first // LIST_ROWS : (first + count) // LIST_ROWS]))
@@ -125,7 +111,17 @@ def tile_attend_gpsquareshares_kernel(tc, query, keys_words, keys_scales, floor,
         val_bytes = sb.tile([P, I], U8, name="val_bytes", align_bytes=64)
         query_bf = cast("query_bf", query_raw)
         gout_bf = cast("gout_bf", gout_raw)
-        val_words = load_words("val_words", vals_words, "query_raw")
+        w = sb.tile([P, 1], F32, name="w", tag="gout_raw")
+        wf4 = n2[:, SHIFT]
+        nc.scalar.activation(w[:], f[:], ACT.Identity, bias=res[:], scale=float(I))
+        nc.scalar.activation(rows[:, :, 2:4], floor_factor[:], ACT.Copy, scale=f[:])
+        nc.scalar.activation(wf4, rows[:, 0, :], ACT.Copy, scale=w[:])
+        for b in range(2):
+            block = slice(2 * b, 2 * b + 2)
+            for dst, src in ((n1_pairs, rows[:, 1 + b, :]), (n2_pairs, wf4)):
+                nc.scalar.activation(dst[:, block, :], src.unsqueeze(1).to_broadcast([P, 2, 4]), ACT.Copy, scale=col(wf4, 2 * b))
+        nc.scalar.activation(n0_pairs[:, 2:4, 2:4], f[:].unsqueeze(2).to_broadcast([P, 2, 2]), ACT.Square, scale=math.sqrt(3.0))
+        val_words = load_words("val_words", vals_words, "val_words")
         gather(key_bytes[:], key_plane[:], 0, I)
         query_mx = quantise("query", query_bf)
         gout_mx = quantise("gout", gout_bf)
@@ -153,7 +149,7 @@ def tile_attend_gpsquareshares_kernel(tc, query, keys_words, keys_scales, floor,
         product(c_v[1][:], gout_mx, val_codes[1][:], val_bytes[:, halves[1]], VAL_ROW)
         product(c_twin[:], gout_mx, val_codes[1][:], val_bytes[:, halves[1]], VAL_ROW)
 
-        r = sb.tile([P, 1], F32, name="r", tag="query_raw")
+        r = sb.tile([P, 1], F32, name="r", tag="val_words")
         q1 = sb.tile([P, COEFS], F32, name="q1")
         u = sb.tile([P, I + COEFS], F32, name="u")
         q2 = u[:, I:]

@@ -48,8 +48,8 @@ def tile_attend_gpsquareshares_kernel(tc, query, keys_words, keys_scales, floor,
         def load_scales(name, src, row, clear):
             plane = sb.tile([P, T], U8, name=name)
             clear.memset(plane[:].bitcast(I32), 0)
-            for quad in range(4):
-                nc.sync.dma_start(plane[32 * quad + row : 32 * quad + row + 4, :].bitcast(I32), src[0, 4 * quad : 4 * quad + 4, :].bitcast(I32))
+            for j in range(4):
+                nc.sync.dma_start(plane[row + j : P : 32, :].bitcast(I32), src[0, j:16:4, :].bitcast(I32))
             return plane
 
         def load_words(name, src, tag):
@@ -187,4 +187,4 @@ def tile_attend_gpsquareshares_kernel(tc, query, keys_words, keys_scales, floor,
         for h in range(2):
             y = sb.tile([P, HALF], F32, name="y%d" % h)
             nc.vector.scalar_tensor_tensor(y[:], x[h][:], col(q2, GAIN), base_sb[:, halves[h]], MULT, ADD)
-            (nc.sync, nc.scalar)[h].dma_start(out[:, halves[h]], y[:])
+            (nc.scalar, nc.sync)[h].dma_start(out[:, halves[h]], y[:])

import math
from contextlib import ExitStack

import concourse.mybir as mybir

D, E, T, I, Q = 512, 512, 2048, 512, 128
FLOPS = 2 * Q * I * (D + E)

F32 = mybir.dt.float32
BF16 = mybir.dt.bfloat16
I32 = mybir.dt.int32
U32 = mybir.dt.uint32
U16 = mybir.dt.uint16
U8 = mybir.dt.uint8
FP8X4 = mybir.dt.float8_e4m3fn_x4
MULT = mybir.AluOpType.mult
ADD = mybir.AluOpType.add
SUB = mybir.AluOpType.subtract
ACT = mybir.ActivationFunctionType

P = 128
PACK = 4
HALF = I // 2
LIST_ROWS = 16
KEY_ROW, VAL_ROW = 0, 4
PAIRS = 16
ONE = 16
SHIFT = slice(18, 22)
SHIFT_S = slice(18, 20)
GAIN = 24
COEFS = 25
TERMS = I + PAIRS + 1


def col(tile, j):
    return tile[:, j : j + 1]


def tile_attend_gpsquareshares_kernel(tc, query, keys_words, keys_scales, floor, reserve, gout, vals_words, vals_scales, base, offs, out):
    nc = tc.nc
    with ExitStack() as ctx:
        sb = ctx.enter_context(tc.tile_pool(name="sb", bufs=1))
        psum = ctx.enter_context(tc.psum_pool(name="psum", bufs=1))

        offsets = sb.tile([P, I // LIST_ROWS], U16, name="offsets")
        nc.sync.dma_start(offsets[:], offs)

        def load_scales(name, src, row, clear):
            plane = sb.tile([P, T], U8, name=name)
            clear.memset(plane[:].bitcast(I32), 0)
            for j in range(4):
                nc.sync.dma_start(plane[row + j : P : 32, :].bitcast(I32), src[0, j:16:4, :].bitcast(I32))
            return plane

        def load_words(name, src, tag):
            words = sb.tile([P, T], I32, name=name, tag=tag)
            nc.sync.dma_start(words[:], src[0].rearrange("p n t -> p (n t)").bitcast(I32))
            return words

        def load_rows(name, src):
            raw = sb.tile([P, PACK, Q], F32, name=name, tag=name)
            nc.sync.dma_start(raw[:], src.rearrange("(p j) q -> p j q", j=PACK))
            return raw

        query_raw = load_rows("query_raw", query)
        gout_raw = load_rows("gout_raw", gout)
        key_plane = load_scales("key_plane", keys_scales, KEY_ROW, nc.gpsimd)
        key_words = load_words("key_words", keys_words, "key_words")
        val_plane = load_scales("val_plane", vals_scales, VAL_ROW, nc.vector)
        f = sb.tile([P, 1], F32, name="f")
        nc.gpsimd.dma_start(f[:], floor)
        res = sb.tile([P, 1], F32, name="res")
        nc.gpsimd.dma_start(res[:], reserve)

        n0 = sb.tile([P, COEFS], F32, name="n0")
        n1 = sb.tile([P, COEFS], F32, name="n1")
        n2 = sb.tile([P, COEFS], F32, name="n2")
        rows = sb.tile([P, 3, 4], F32, name="rows")
        floor_factor = sb.tile([P, 3, 2], F32, name="floor_factor")
        n0_pairs, n1_pairs, n2_pairs = [n[:, :PAIRS].rearrange("p (a b) -> p a b", a=4) for n in (n0, n1, n2)]
        nc.vector.memset(n0[:], 0.0)
        nc.vector.memset(n0_pairs[:, 0:2, 0:2], -0.5)
        nc.vector.memset(col(n0, ONE), 1.0)
        nc.vector.memset(n1[:, PAIRS:], 0.0)
        nc.vector.memset(n1[:, SHIFT_S], 0.5)
        nc.vector.memset(n2[:, PAIRS:], 0.0)
        nc.vector.memset(col(n2, GAIN), float(2**21))
        for j, (first, second) in enumerate(((0.5, 1.0), (-1.0, -3.0), (-1.5, -4.0))):
            nc.vector.memset(rows[:, j, 0:2], first)
            nc.vector.memset(floor_factor[:, j, :], second)

        def gather(dst, window, first, count):
            nc.vector.tensor_copy(dst, window.indirect(offsets[:, first // LIST_ROWS : (first + count) // LIST_ROWS]))

        def cast(name, raw):
            grouped = sb.tile([P, Q, PACK], BF16, name=name, align_bytes=64)
            nc.scalar.activation(grouped[:], raw[:].rearrange("p j q -> p q j"), ACT.Copy)
            return grouped

        def quantise(name, grouped):
            codes = sb.tile([P, Q], U32, name=name + "_codes", align_bytes=64)
            scales = sb.tile([P, Q], U8, name=name + "_scales", align_bytes=64)
            nc.vector.quantize_mx(out=codes[:].bitcast(FP8X4), scales=scales[:], in_=grouped[:].rearrange("p q j -> p (q j)"))
            return codes, scales

        def product(dst, lhs, words, plane, row):
            nc.tensor.matmul_mx(out=dst, lhsT=lhs[0][:].bitcast(FP8X4), lhsT_scale=lhs[1][:], rhs=words.bitcast(FP8X4), rhs_scale=plane[row:P, :], start=True, stop=True)

        key_bytes = sb.tile([P, I], U8, name="key_bytes", align_bytes=64)
        key_codes = sb.tile([P, I], U32, name="key_codes", align_bytes=64)
        val_bytes = sb.tile([P, I], U8, name="val_bytes", align_bytes=64)
        query_bf = cast("query_bf", query_raw)
        gout_bf = cast("gout_bf", gout_raw)
        w = sb.tile([P, 1], F32, name="w", tag="gout_raw")
        wf4 = n2[:, SHIFT]
        nc.scalar.activation(w[:], f[:], ACT.Identity, bias=res[:], scale=float(I))
        nc.scalar.activation(rows[:, :, 2:4], floor_factor[:], ACT.Copy, scale=f[:])
        nc.scalar.activation(wf4, rows[:, 0, :], ACT.Copy, scale=w[:])
        for b in range(2):
            block = slice(2 * b, 2 * b + 2)
            for dst, src in ((n1_pairs, rows[:, 1 + b, :]), (n2_pairs, wf4)):
                nc.scalar.activation(dst[:, block, :], src.unsqueeze(1).to_broadcast([P, 2, 4]), ACT.Copy, scale=col(wf4, 2 * b))
        nc.scalar.activation(n0_pairs[:, 2:4, 2:4], f[:].unsqueeze(2).to_broadcast([P, 2, 2]), ACT.Square, scale=math.sqrt(3.0))
        val_words = load_words("val_words", vals_words, "val_words")
        gather(key_bytes[:], key_plane[:], 0, I)
        query_mx = quantise("query", query_bf)
        gout_mx = quantise("gout", gout_bf)
        gather(key_codes[:], key_words[:].bitcast(U32), 0, I)
        base_sb = sb.tile([P, I], F32, name="base_sb", tag="key_words")
        nc.sync.dma_start(base_sb[:], base)
        a = psum.tile([P, I], F32, name="a")
        product(a[:], query_mx, key_codes[:], key_bytes[:], KEY_ROW)
        gather(val_bytes[:], val_plane[:], 0, I)

        s = sb.tile([P, I], F32, name="s")
        s0 = sb.tile([P, 1], F32, name="s0")
        nc.scalar.activation(s[:], a[:], ACT.Square, accum_out=s0[:])
        z = sb.tile([P, 1], F32, name="z")
        nc.scalar.activation(z[:], s0[:], ACT.Identity, bias=w[:])

        halves = [slice(h * HALF, (h + 1) * HALF) for h in range(2)]
        val_codes = [sb.tile([P, HALF], U32, name="val_codes%d" % h, align_bytes=64) for h in range(2)]
        for h in range(2):
            gather(val_codes[h][:], val_words[:].bitcast(U32), h * HALF, HALF)
        c_v = [psum.tile([P, HALF], F32, name="c%d" % h) for h in range(2)]
        c_twin = psum.tile([P, HALF], F32, name="c_twin")
        c_s = [c_v[0], c_twin]
        product(c_v[0][:], gout_mx, val_codes[0][:], val_bytes[:, halves[0]], VAL_ROW)
        product(c_v[1][:], gout_mx, val_codes[1][:], val_bytes[:, halves[1]], VAL_ROW)
        product(c_twin[:], gout_mx, val_codes[1][:], val_bytes[:, halves[1]], VAL_ROW)

        r = sb.tile([P, 1], F32, name="r", tag="val_words")
        q1 = sb.tile([P, COEFS], F32, name="q1")
        u = sb.tile([P, I + COEFS], F32, name="u")
        q2 = u[:, I:]
        sums = sb.tile([P, 4], F32, name="sums")
        c = sb.tile([P, TERMS], F32, name="c")
        nc.vector.reciprocal(r[:], z[:])
        for h in range(2):
            nc.vector.scalar_tensor_tensor(u[:, halves[h]], c_v[h][:], 2.0, s[:, halves[h]], MULT, MULT, accum_out=col(sums, h))
            nc.scalar.activation(c[:, halves[h]], c_s[h][:], ACT.Copy, accum_out=col(sums, 2 + h))
            if h == 0:
                nc.vector.scalar_tensor_tensor(q1[:], n2[:], r[:], n1[:], MULT, ADD)
                nc.vector.scalar_tensor_tensor(q2, q1[:], r[:], n0[:], MULT, ADD)
        level_terms = sb.tile([P, TERMS], F32, name="level_terms")
        nc.vector.scalar_tensor_tensor(level_terms[:, :HALF], c[:, :HALF], 1.0, u[:, :HALF], MULT, MULT, accum_out=col(c, I + ONE))
        nc.vector.scalar_tensor_tensor(
            c[:, I : I + PAIRS].rearrange("p (a b) -> p a b", a=4),
            sums[:].unsqueeze(2).to_broadcast([P, 4, 4]),
            r[:],
            sums[:].unsqueeze(1).to_broadcast([P, 4, 4]),
            MULT,
            MULT,
        )
        shift = sb.tile([P, 1], F32, name="shift")
        shift_terms = sb.tile([P, 4], F32, name="shift_terms")
        nc.vector.scalar_tensor_tensor(shift_terms[:], sums[:], r[:], q1[:, SHIFT], MULT, MULT, accum_out=shift[:])
        level = sb.tile([P, 1], F32, name="level")
        nc.vector.scalar_tensor_tensor(level_terms[:, HALF:], c[:, HALF:], r[:], u[:, HALF:TERMS], MULT, MULT, accum_out=level[:])

        x = []
        for h in range(2):
            t = sb.tile([P, HALF], F32, name="t%d" % h)
            nc.scalar.activation(t[:], c[:, halves[h]], ACT.Square, bias=shift[:], scale=-1.0)
            x.append(sb.tile([P, HALF], F32, name="x%d" % h))
            nc.vector.scalar_tensor_tensor(x[h][:], t[:], level[:], a[:, halves[h]], SUB, MULT)
        for h in range(2):
            y = sb.tile([P, HALF], F32, name="y%d" % h)
            nc.vector.scalar_tensor_tensor(y[:], x[h][:], col(q2, GAIN), base_sb[:, halves[h]], MULT, ADD)
            (nc.scalar, nc.sync)[h].dma_start(out[:, halves[h]], y[:])
